import numpy as np
import ml_dtypes


def mxq(x, axis, fmt="e4m3"):
    dtype, down = {"e4m3": (ml_dtypes.float8_e4m3fn, 7), "e5m2": (ml_dtypes.float8_e5m2, 14)}[fmt]
    v = np.moveaxis(np.asarray(x, np.float32).astype(ml_dtypes.bfloat16).astype(np.float64), axis, -1)
    blocks = v.reshape(v.shape[:-1] + (-1, 32))
    amax = np.abs(blocks).max(-1, keepdims=True)
    byte = np.maximum(np.where(amax > 0, np.frexp(amax)[1] - 1 + 127, 0) - down, 1)
    scale = np.exp2(byte - 127.0)
    codes = (blocks / scale).astype(np.float32).astype(dtype).astype(np.float64)
    return np.moveaxis((codes * scale).reshape(v.shape), -1, axis)


WIDE = False


def mx_kscale(k):
    if not WIDE:
        return np.ones(k)
    levels = np.array([10, -10, 5, -5, 0])
    if k % 512:
        return np.exp2(np.random.permutation(np.resize(levels, k // 32))).repeat(32)
    a = np.empty((k // 512, 16))
    for p in range(k // 512):
        a[p, :8] = np.random.permutation(np.resize(levels, 8))
        for g in range(8):
            far = levels[np.abs(levels - a[p, g]) >= 10]
            a[p, g + 8] = far[np.random.randint(len(far))]
    return np.exp2(a.ravel()).repeat(32)


def f64(x):
    return np.asarray(x).astype(np.float64)


def striped(idx):
    return np.tile(idx.reshape(-1, 16).T, (8, 1)).astype(np.uint16)


def unstriped(offs):
    return offs[:16].T.reshape(-1).astype(np.int64)


def striped8(idx):
    return np.concatenate([x.reshape(-1, 16).T for x in idx]).astype(np.uint16)


def runs(offs, k):
    lists = np.stack([offs[16 * r : 16 * r + 16].T.reshape(-1) for r in range(8)]).astype(np.int64)
    return lists[np.arange(k) % 512 // 64]


def pack_weight(w):
    k, n = w.shape
    w = f64(np.asarray(w, np.float32).astype(ml_dtypes.bfloat16)).reshape(k // 32, 32, n)
    amax = np.abs(w).max(1)
    byte = np.clip(np.where(amax > 0, np.frexp(amax)[1] - 1 + 127 - 7, 1), 1, 254)
    scaled = (w * np.exp2(127.0 - byte)[:, None, :]).reshape(k, n).astype(np.float32)
    words = np.ascontiguousarray(scaled.reshape(k // 512, 128, 4, n).transpose(0, 1, 3, 2)).astype(ml_dtypes.float8_e4m3fn).view(np.uint8)
    return words, np.ascontiguousarray(byte.astype(np.uint8).reshape(k // 512, 16, n))


def unpack_weight(words, scales):
    g, p, n, _ = words.shape
    vals = np.ascontiguousarray(words).view(ml_dtypes.float8_e4m3fn).astype(np.float64) * np.repeat(np.exp2(scales.astype(np.float64) - 127.0), 8, axis=1)[..., None]
    return vals.transpose(0, 1, 3, 2).reshape(g * 512, n)


def relu(v):
    return np.maximum(v, 0.0)


K, T, S, N, H = 512, 2048, 256, 512, 512


def setup_inputs():
    n = np.random.standard_normal
    s = mx_kscale(K)[:, None]
    u = mx_kscale(H)
    packed_xT = pack_weight(n((K, T)) * s)
    return {
        "x_words": packed_xT[0],
        "x_scales": packed_xT[1],
        "w1": (n((K, H)) / np.sqrt(K) / s).astype(np.float32),
        "gn": (np.random.uniform(0.5, 1.5, (H, 1)) * u[:, None]).astype(np.float32),
        "w2": (n((H, N)) / np.sqrt(H) / u[:, None]).astype(np.float32),
        "offs": striped8(np.random.randint(0, T, (8, S))),
        "n1": striped(np.random.permutation(S)),
        "n2": striped(np.random.permutation(S)),
        "n3": striped(np.random.permutation(S)),
    }


def reference(x_words, x_scales, w1, gn, w2, offs, n1, n2, n3):
    xq = unpack_weight(x_words, x_scales)[np.arange(K)[:, None], runs(offs, K)]
    y = mxq(f64(w1), 0, "e4m3").T @ xq
    z = f64(gn) * (y / (np.abs(y[:, unstriped(n1)]) + 0.5))
    h = mxq(f64(w2), 0, "e4m3").T @ mxq(z, 0, "e4m3")
    return relu(h - h[:, unstriped(n2)]) + 0.5 * (relu(h[:, unstriped(n3)] - h))

@@ -1,0 +1,199 @@
+from contextlib import ExitStack
+
+import concourse.mybir as mybir
+
+F32 = mybir.dt.float32
+BF16 = mybir.dt.bfloat16
+I32 = mybir.dt.int32
+U32 = mybir.dt.uint32
+U16 = mybir.dt.uint16
+U8 = mybir.dt.uint8
+FP8X4 = mybir.dt.float8_e4m3fn_x4
+ALU = mybir.AluOpType
+ACT = mybir.ActivationFunctionType
+
+P = 128
+PACK = 4
+T = 2048
+S = 256
+HALF = S // 2
+WIDTH = 512
+TILES = WIDTH // P
+SPARE = 8
+FLOPS = 2 * 2 * WIDTH * WIDTH * S
+
+
+def tile_picked_hashnormhinge_none_p_kernel(
+    tc, x_words, x_scales, w1, gn, w2, offs, n1, n2, n3, out
+):
+    nc = tc.nc
+    with ExitStack() as ctx:
+        keep = ctx.enter_context(tc.tile_pool(name="keep", bufs=1))
+        psum = ctx.enter_context(tc.psum_pool(name="psum", bufs=1))
+
+        lists = {}
+        for name, source in (("offs", offs), ("n1", n1), ("n2", n2), ("n3", n3)):
+            lists[name] = keep.tile([P, S // 16], U16, name=name + "_sb")
+            nc.sync.dma_start(lists[name][:], source)
+
+        scale_table = keep.tile([P, T], U8, align_bytes=64)
+        nc.vector.memset(scale_table[:].bitcast(I32), 0)
+        for row in range(2):
+            nc.scalar.dma_start(
+                scale_table[row:P:16, :].bitcast(I32), x_scales[0][row:16:2, :].bitcast(I32)
+            )
+        gain = keep.tile([P, PACK], F32)
+        nc.scalar.dma_start(gain[:], gn.rearrange("(p t) o -> p (t o)", t=PACK))
+
+        w1_raw = keep.tile([P, PACK, WIDTH], F32)
+        nc.sync.dma_start(w1_raw[:], w1.rearrange("(p j) c -> p j c", j=PACK))
+        word_table = keep.tile([P, T], U32, align_bytes=64)
+        nc.sync.dma_start(
+            word_table[:].bitcast(I32), x_words[0].rearrange("p n t -> p (n t)").bitcast(I32)
+        )
+        w2_raw = keep.tile([P, PACK, WIDTH], F32)
+        nc.sync.dma_start(w2_raw[:], w2.rearrange("(p j) c -> p j c", j=PACK))
+
+        half = keep.tile([P, 1], F32)
+        nc.gpsimd.memset(half[:], 0.5)
+        h_rows = []
+        for m in range(TILES):
+            h_row = keep.tile([P, S + SPARE], F32, name="h_row%d" % m)
+            nc.gpsimd.memset(h_row[:, S:], 0.0)
+            h_rows.append(h_row)
+
+        picked_scales = keep.tile([P, S], U8, align_bytes=64)
+        nc.vector.tensor_copy(picked_scales[:], scale_table[:].indirect(lists["offs"][:]))
+        x_plane = keep.tile([P, S], U8, align_bytes=64)
+        nc.vector.tensor_copy(x_plane[:].bitcast(I32), picked_scales[:].bitcast(I32))
+        for row in range(2):
+            nc.scalar.dma_start(
+                x_plane[2 + row : P : 32, :].bitcast(I32),
+                picked_scales[16 + row : P : 32, :].bitcast(I32),
+            )
+
+        w1_bf = keep.tile([P, PACK * WIDTH], BF16, align_bytes=64)
+        nc.vector.tensor_copy(
+            w1_bf[:].rearrange("p (t m j) -> p m j t", t=PACK, j=PACK),
+            w1_raw[:].rearrange("p j (m t) -> p m j t", t=PACK),
+        )
+        w1_codes = keep.tile([P, WIDTH], U32, align_bytes=64)
+        w1_plane = keep.tile([P, WIDTH], U8, align_bytes=64)
+        nc.vector.quantize_mx(out=w1_codes[:].bitcast(FP8X4), scales=w1_plane[:], in_=w1_bf[:])
+
+        x_codes = keep.tile([P, S], U32, align_bytes=64)
+        nc.vector.tensor_copy(x_codes[:], word_table[:].indirect(lists["offs"][:]))
+
+        size = keep.tile([P, PACK, S], F32)
+        y_banks = []
+        for a in range(2):
+            cols = slice(a * HALF, (a + 1) * HALF)
+            y_bank = psum.tile([P, PACK, HALF], F32, name="y_bank%d" % a)
+            for t in range(PACK):
+                rows = slice(t * P, (t + 1) * P)
+                nc.tensor.matmul_mx(
+                    out=y_bank[:, t, :],
+                    lhsT=w1_codes[:, rows].bitcast(FP8X4),
+                    lhsT_scale=w1_plane[:, rows],
+                    rhs=x_codes[:, cols].bitcast(FP8X4),
+                    rhs_scale=x_plane[:, cols],
+                    start=True,
+                    stop=True,
+                )
+            nc.scalar.activation(size[:, :, cols], y_bank[:], ACT.Abs)
+            y_banks.append(y_bank)
+
+        root = keep.tile([P, PACK, S], F32)
+        factor = keep.tile([P, PACK, S], F32, align_bytes=64, tag="factor")
+        for t in range(PACK):
+            nc.scalar.activation(root[:, t, :], size[:, t, :], ACT.Abs_reciprocal_sqrt, bias=half[:])
+            nc.vector.scalar_tensor_tensor(
+                factor[:, t, :], root[:, t, :], gain[:, t : t + 1], root[:, t, :], ALU.mult, ALU.mult
+            )
+
+        w2_codes = keep.tile([P, WIDTH], U32, align_bytes=64)
+        w2_plane = keep.tile([P, WIDTH], U8, align_bytes=64)
+
+        def interleave_w2(copy, staged, first):
+            for m in range(2):
+                rows = slice((first + m) * P, (first + m + 1) * P)
+                copy(
+                    staged[:, m * P : (m + 1) * P, :].rearrange("p (c i) j -> p c j i", i=4),
+                    w2_raw[:, :, rows].rearrange("p j (c i) -> p c j i", i=4),
+                )
+
+        def quantize_w2(staged, first):
+            rows = slice(first * P, (first + 2) * P)
+            nc.vector.quantize_mx(
+                out=w2_codes[:, rows].bitcast(FP8X4),
+                scales=w2_plane[:, rows],
+                in_=staged[:].rearrange("p c j -> p (c j)"),
+            )
+
+        def second_product(m, cols):
+            rows = slice(m * P, (m + 1) * P)
+            nc.tensor.matmul_mx(
+                out=h_banks[m][:, cols],
+                lhsT=w2_codes[:, rows].bitcast(FP8X4),
+                lhsT_scale=w2_plane[:, rows],
+                rhs=z_codes[:, cols].bitcast(FP8X4),
+                rhs_scale=z_plane[:, cols],
+                start=True,
+                stop=True,
+            )
+
+        w2_low = keep.tile([P, 2 * P, PACK], BF16, align_bytes=64)
+        interleave_w2(nc.vector.tensor_copy, w2_low, 0)
+        quantize_w2(w2_low, 0)
+
+        z_codes = keep.tile([P, S], U32, align_bytes=64)
+        z_plane = keep.tile([P, S], U8, align_bytes=64)
+        h_banks = [psum.tile([P, S], F32, name="h_bank%d" % m) for m in range(TILES)]
+        for a in range(2):
+            cols = slice(a * HALF, (a + 1) * HALF)
+            picked = keep.tile([P, PACK, HALF], F32, name="picked%d" % a)
+            for t in range(PACK):
+                nc.scalar.activation(
+                    picked[:, t, :],
+                    factor[:, t, :].indirect(lists["n1"][:, a * 8 : (a + 1) * 8]),
+                    ACT.Copy,
+                )
+            z_bf = keep.tile([P, HALF, PACK], BF16, align_bytes=64, name="z_bf")
+            nc.vector.tensor_tensor(
+                z_bf[:].rearrange("p (c i) t -> p c t i", i=4),
+                y_banks[a][:].rearrange("p t (c i) -> p c t i", i=4),
+                picked[:].rearrange("p t (c i) -> p c t i", i=4),
+                ALU.mult,
+            )
+            nc.vector.quantize_mx(
+                out=z_codes[:, cols].bitcast(FP8X4),
+                scales=z_plane[:, cols],
+                in_=z_bf[:].rearrange("p c t -> p (c t)"),
+            )
+            for m in range(2):
+                second_product(m, cols)
+
+        w2_high = keep.tile([P, 2 * P, PACK], BF16, align_bytes=64, tag="factor")
+        interleave_w2(nc.scalar.copy, w2_high, 2)
+        for m in range(2):
+            nc.vector.tensor_copy(h_rows[m][:, :S], h_banks[m][:])
+        quantize_w2(w2_high, 2)
+        for m in range(2, TILES):
+            second_product(m, slice(0, S))
+            nc.vector.tensor_copy(h_rows[m][:, :S], h_banks[m][:])
+
+        for m in range(TILES):
+            h_own = h_rows[m][:, :S]
+            above = keep.tile([P, S], F32, name="above%d" % m)
+            nc.scalar.activation(above[:], h_rows[m][:].indirect(lists["n3"][:]), ACT.Copy)
+            below = keep.tile([P, S], F32, name="below%d" % m)
+            nc.scalar.activation(below[:], h_rows[m][:].indirect(lists["n2"][:]), ACT.Copy)
+            rise = keep.tile([P, S], F32, name="rise%d" % m)
+            nc.vector.tensor_tensor(rise[:], above[:], h_own, ALU.subtract)
+            pull = keep.tile([P, S], F32, name="pull%d" % m)
+            nc.vector.tensor_scalar(pull[:], rise[:], 0.0, 0.5, ALU.max, ALU.mult)
+            drop = keep.tile([P, S], F32, name="drop%d" % m)
+            nc.vector.tensor_tensor(drop[:], h_own, below[:], ALU.subtract)
+            result = keep.tile([P, S], F32, name="result%d" % m)
+            nc.vector.scalar_tensor_tensor(result[:], drop[:], 0.0, pull[:], ALU.max, ALU.add)
+            nc.sync.dma_start(out[m * P : (m + 1) * P, :], result[:])

@@ -32,18 +32,18 @@ def tile_picked_hashnormhinge_none_p_kernel(
         psum = ctx.enter_context(tc.psum_pool(name="psum", bufs=1))
 
         lists = {}
-        for name, source in (("offs", offs), ("n1", n1), ("n2", n2), ("n3", n3)):
+
+        def load_list(name, source):
             lists[name] = keep.tile([P, S // 16], U16, name=name + "_sb")
             nc.sync.dma_start(lists[name][:], source)
 
-        scale_table = keep.tile([P, T], U8, align_bytes=64)
-        nc.vector.memset(scale_table[:].bitcast(I32), 0)
-        for row in range(2):
-            nc.scalar.dma_start(
-                scale_table[row:P:16, :].bitcast(I32), x_scales[0][row:16:2, :].bitcast(I32)
-            )
-        gain = keep.tile([P, PACK], F32)
-        nc.scalar.dma_start(gain[:], gn.rearrange("(p t) o -> p (t o)", t=PACK))
+        load_list("offs", offs)
+        load_list("n1", n1)
+
+        scale_table = keep.tile([P, T], U8, align_bytes=64, tag="scale_table")
+        nc.gpsimd.memset(scale_table[:].bitcast(I32)[:, :384], 0)
+        nc.vector.memset(scale_table[:].bitcast(I32)[:, 384:], 0)
+        nc.sync.dma_start(scale_table[0:P:8, :].bitcast(I32), x_scales[0].bitcast(I32))
 
         w1_raw = keep.tile([P, PACK, WIDTH], F32)
         nc.sync.dma_start(w1_raw[:], w1.rearrange("(p j) c -> p j c", j=PACK))
@@ -51,32 +51,46 @@ def tile_picked_hashnormhinge_none_p_kernel(
         nc.sync.dma_start(
             word_table[:].bitcast(I32), x_words[0].rearrange("p n t -> p (n t)").bitcast(I32)
         )
-        w2_raw = keep.tile([P, PACK, WIDTH], F32)
-        nc.sync.dma_start(w2_raw[:], w2.rearrange("(p j) c -> p j c", j=PACK))
+        load_list("n3", n3)
+        load_list("n2", n2)
 
         half = keep.tile([P, 1], F32)
         nc.gpsimd.memset(half[:], 0.5)
+        warm = keep.tile([P, 1], F32)
+        nc.scalar.activation(warm[:], half[:], ACT.Abs_reciprocal_sqrt, bias=half[:])
         h_rows = []
         for m in range(TILES):
             h_row = keep.tile([P, S + SPARE], F32, name="h_row%d" % m)
             nc.gpsimd.memset(h_row[:, S:], 0.0)
             h_rows.append(h_row)
 
-        picked_scales = keep.tile([P, S], U8, align_bytes=64)
+        picked_scales = keep.tile([P, S], U8, align_bytes=64, tag="picked_scales")
         nc.vector.tensor_copy(picked_scales[:], scale_table[:].indirect(lists["offs"][:]))
         x_plane = keep.tile([P, S], U8, align_bytes=64)
-        nc.vector.tensor_copy(x_plane[:].bitcast(I32), picked_scales[:].bitcast(I32))
-        for row in range(2):
-            nc.scalar.dma_start(
-                x_plane[2 + row : P : 32, :].bitcast(I32),
-                picked_scales[16 + row : P : 32, :].bitcast(I32),
+        nc.vector.memset(x_plane[:].bitcast(I32), 0)
+        for q in range(4):
+            rows = slice(32 * q, 32 * q + 1)
+            nc.vector.tensor_copy(x_plane[rows, :].bitcast(I32), picked_scales[rows, :].bitcast(I32))
+        for row in range(1, 4):
+            nc.sync.dma_start(
+                x_plane[row:P:32, :].bitcast(I32),
+                picked_scales[8 * row : P : 32, :].bitcast(I32),
             )
 
+        w2_rows = w2.rearrange("(p j) c -> p j c", j=PACK)
+        w2_raw = keep.tile([P, 2, PACK, 2 * P], F32, align_bytes=64, tag="scale_table")
+        for b in range(2):
+            nc.sync.dma_start(w2_raw[:, b], w2_rows[:, :, b * 2 * P : (b + 1) * 2 * P])
+
+        gain = keep.tile([P, PACK], F32, align_bytes=64, tag="picked_scales")
+        nc.sync.dma_start(gain[:], gn.rearrange("(p t) o -> p (t o)", t=PACK))
+
         w1_bf = keep.tile([P, PACK * WIDTH], BF16, align_bytes=64)
-        nc.vector.tensor_copy(
-            w1_bf[:].rearrange("p (t m j) -> p m j t", t=PACK, j=PACK),
-            w1_raw[:].rearrange("p j (m t) -> p m j t", t=PACK),
-        )
+        for copy, share in ((nc.scalar.copy, slice(0, 40)), (nc.vector.tensor_copy, slice(40, P))):
+            copy(
+                w1_bf[:].rearrange("p (t m j) -> p m j t", t=PACK, j=PACK)[:, share],
+                w1_raw[:].rearrange("p j (m t) -> p m j t", t=PACK)[:, share],
+            )
         w1_codes = keep.tile([P, WIDTH], U32, align_bytes=64)
         w1_plane = keep.tile([P, WIDTH], U8, align_bytes=64)
         nc.vector.quantize_mx(out=w1_codes[:].bitcast(FP8X4), scales=w1_plane[:], in_=w1_bf[:])
@@ -103,12 +117,21 @@ def tile_picked_hashnormhinge_none_p_kernel(
             nc.scalar.activation(size[:, :, cols], y_bank[:], ACT.Abs)
             y_banks.append(y_bank)
 
-        root = keep.tile([P, PACK, S], F32)
-        factor = keep.tile([P, PACK, S], F32, align_bytes=64, tag="factor")
+        root = keep.tile([P, PACK, S], F32, tag="root")
+        factors = [keep.tile([P, S], F32, name="factor%d" % t) for t in range(PACK)]
         for t in range(PACK):
-            nc.scalar.activation(root[:, t, :], size[:, t, :], ACT.Abs_reciprocal_sqrt, bias=half[:])
+            if t % 2 == 0:
+                width = HALF if t == 0 else S
+                for first in range(0, S, width):
+                    part = slice(first, first + width)
+                    nc.scalar.activation(
+                        root[:, t : t + 2, part],
+                        size[:, t : t + 2, part],
+                        ACT.Abs_reciprocal_sqrt,
+                        bias=half[:],
+                    )
             nc.vector.scalar_tensor_tensor(
-                factor[:, t, :], root[:, t, :], gain[:, t : t + 1], root[:, t, :], ALU.mult, ALU.mult
+                factors[t][:], root[:, t, :], gain[:, t : t + 1], root[:, t, :], ALU.mult, ALU.mult
             )
 
         w2_codes = keep.tile([P, WIDTH], U32, align_bytes=64)
@@ -116,10 +139,10 @@ def tile_picked_hashnormhinge_none_p_kernel(
 
         def interleave_w2(copy, staged, first):
             for m in range(2):
-                rows = slice((first + m) * P, (first + m + 1) * P)
+                rows = slice(m * P, (m + 1) * P)
                 copy(
                     staged[:, m * P : (m + 1) * P, :].rearrange("p (c i) j -> p c j i", i=4),
-                    w2_raw[:, :, rows].rearrange("p j (c i) -> p c j i", i=4),
+                    w2_raw[:, first // 2, :, rows].rearrange("p j (c i) -> p c j i", i=4),
                 )
 
         def quantize_w2(staged, first):
@@ -145,17 +168,20 @@ def tile_picked_hashnormhinge_none_p_kernel(
         w2_low = keep.tile([P, 2 * P, PACK], BF16, align_bytes=64)
         interleave_w2(nc.vector.tensor_copy, w2_low, 0)
         quantize_w2(w2_low, 0)
+        w2_high = keep.tile([P, 2 * P, PACK], BF16, align_bytes=64)
+        interleave_w2(nc.vector.tensor_copy, w2_high, 2)
+        quantize_w2(w2_high, 2)
 
         z_codes = keep.tile([P, S], U32, align_bytes=64)
         z_plane = keep.tile([P, S], U8, align_bytes=64)
         h_banks = [psum.tile([P, S], F32, name="h_bank%d" % m) for m in range(TILES)]
         for a in range(2):
             cols = slice(a * HALF, (a + 1) * HALF)
-            picked = keep.tile([P, PACK, HALF], F32, name="picked%d" % a)
+            picked = keep.tile([P, PACK, HALF], F32, name="picked%d" % a, tag=("picked", "root")[a])
             for t in range(PACK):
                 nc.scalar.activation(
                     picked[:, t, :],
-                    factor[:, t, :].indirect(lists["n1"][:, a * 8 : (a + 1) * 8]),
+                    factors[t][:].indirect(lists["n1"][:, a * 8 : (a + 1) * 8]),
                     ACT.Copy,
                 )
             z_bf = keep.tile([P, HALF, PACK], BF16, align_bytes=64, name="z_bf")
@@ -170,30 +196,34 @@ def tile_picked_hashnormhinge_none_p_kernel(
                 scales=z_plane[:, cols],
                 in_=z_bf[:].rearrange("p c t -> p (c t)"),
             )
-            for m in range(2):
+            for m in range(TILES):
                 second_product(m, cols)
 
-        w2_high = keep.tile([P, 2 * P, PACK], BF16, align_bytes=64, tag="factor")
-        interleave_w2(nc.scalar.copy, w2_high, 2)
-        for m in range(2):
-            nc.vector.tensor_copy(h_rows[m][:, :S], h_banks[m][:])
-        quantize_w2(w2_high, 2)
-        for m in range(2, TILES):
-            second_product(m, slice(0, S))
-            nc.vector.tensor_copy(h_rows[m][:, :S], h_banks[m][:])
+        for m in range(TILES):
+            copy = nc.scalar.copy if m == 0 else nc.vector.tensor_copy
+            copy(h_rows[m][:, :S], h_banks[m][:])
 
         for m in range(TILES):
             h_own = h_rows[m][:, :S]
             above = keep.tile([P, S], F32, name="above%d" % m)
             nc.scalar.activation(above[:], h_rows[m][:].indirect(lists["n3"][:]), ACT.Copy)
-            below = keep.tile([P, S], F32, name="below%d" % m)
-            nc.scalar.activation(below[:], h_rows[m][:].indirect(lists["n2"][:]), ACT.Copy)
             rise = keep.tile([P, S], F32, name="rise%d" % m)
             nc.vector.tensor_tensor(rise[:], above[:], h_own, ALU.subtract)
             pull = keep.tile([P, S], F32, name="pull%d" % m)
             nc.vector.tensor_scalar(pull[:], rise[:], 0.0, 0.5, ALU.max, ALU.mult)
+            below = keep.tile([P, S], F32, name="below%d" % m)
             drop = keep.tile([P, S], F32, name="drop%d" % m)
-            nc.vector.tensor_tensor(drop[:], h_own, below[:], ALU.subtract)
             result = keep.tile([P, S], F32, name="result%d" % m)
-            nc.vector.scalar_tensor_tensor(result[:], drop[:], 0.0, pull[:], ALU.max, ALU.add)
-            nc.sync.dma_start(out[m * P : (m + 1) * P, :], result[:])
+            width = HALF if m == TILES - 1 else S
+            for first in range(0, S, width):
+                cols = slice(first, first + width)
+                entries = lists["n2"][:, first // 16 : (first + width) // 16]
+                if first:
+                    nc.vector.tensor_copy(below[:, cols], h_rows[m][:].indirect(entries))
+                else:
+                    nc.scalar.activation(below[:, cols], h_rows[m][:].indirect(entries), ACT.Copy)
+                nc.vector.tensor_tensor(drop[:, cols], h_own[:, cols], below[:, cols], ALU.subtract)
+                nc.vector.scalar_tensor_tensor(
+                    result[:, cols], drop[:, cols], 0.0, pull[:, cols], ALU.max, ALU.add
+                )
+                nc.sync.dma_start(out[m * P : (m + 1) * P, cols], result[:, cols])

@@ -200,7 +200,7 @@ def tile_picked_hashnormhinge_none_p_kernel(
                 second_product(m, cols)
 
         for m in range(TILES):
-            copy = nc.scalar.copy if m == 0 else nc.vector.tensor_copy
+            copy = nc.scalar.copy if m < 2 else nc.vector.tensor_copy
             copy(h_rows[m][:, :S], h_banks[m][:])
 
         for m in range(TILES):
@@ -214,14 +214,16 @@ def tile_picked_hashnormhinge_none_p_kernel(
             below = keep.tile([P, S], F32, name="below%d" % m)
             drop = keep.tile([P, S], F32, name="drop%d" % m)
             result = keep.tile([P, S], F32, name="result%d" % m)
+            window = h_rows[m][:]
+            if m == 0:
+                nc.scalar.activation(below[:, :HALF], window.indirect(lists["n2"][:, :8]), ACT.Copy)
+                nc.vector.tensor_copy(below[:, HALF:], window.indirect(lists["n2"][:, 8:]))
             width = HALF if m == TILES - 1 else S
             for first in range(0, S, width):
                 cols = slice(first, first + width)
-                entries = lists["n2"][:, first // 16 : (first + width) // 16]
-                if first:
-                    nc.vector.tensor_copy(below[:, cols], h_rows[m][:].indirect(entries))
-                else:
-                    nc.scalar.activation(below[:, cols], h_rows[m][:].indirect(entries), ACT.Copy)
+                if m > 0:
+                    entries = lists["n2"][:, first // 16 : (first + width) // 16]
+                    nc.scalar.activation(below[:, cols], window.indirect(entries), ACT.Copy)
                 nc.vector.tensor_tensor(drop[:, cols], h_own[:, cols], below[:, cols], ALU.subtract)
                 nc.vector.scalar_tensor_tensor(
                     result[:, cols], drop[:, cols], 0.0, pull[:, cols], ALU.max, ALU.add

from contextlib import ExitStack

import concourse.mybir as mybir

F32 = mybir.dt.float32
BF16 = mybir.dt.bfloat16
I32 = mybir.dt.int32
U32 = mybir.dt.uint32
U16 = mybir.dt.uint16
U8 = mybir.dt.uint8
FP8X4 = mybir.dt.float8_e4m3fn_x4
ALU = mybir.AluOpType
ACT = mybir.ActivationFunctionType

P = 128
PACK = 4
T = 2048
S = 256
HALF = S // 2
WIDTH = 512
TILES = WIDTH // P
SPARE = 8
FLOPS = 2 * 2 * WIDTH * WIDTH * S


def tile_picked_hashnormhinge_none_p_kernel(
    tc, x_words, x_scales, w1, gn, w2, offs, n1, n2, n3, out
):
    nc = tc.nc
    with ExitStack() as ctx:
        keep = ctx.enter_context(tc.tile_pool(name="keep", bufs=1))
        psum = ctx.enter_context(tc.psum_pool(name="psum", bufs=1))

        lists = {}

        def load_list(name, source):
            lists[name] = keep.tile([P, S // 16], U16, name=name + "_sb")
            nc.sync.dma_start(lists[name][:], source)

        load_list("offs", offs)
        load_list("n1", n1)

        scale_table = keep.tile([P, T], U8, align_bytes=64, tag="scale_table")
        nc.gpsimd.memset(scale_table[:].bitcast(I32)[:, :384], 0)
        nc.vector.memset(scale_table[:].bitcast(I32)[:, 384:], 0)
        nc.sync.dma_start(scale_table[0:P:8, :].bitcast(I32), x_scales[0].bitcast(I32))

        w1_raw = keep.tile([P, PACK, WIDTH], F32)
        nc.sync.dma_start(w1_raw[:], w1.rearrange("(p j) c -> p j c", j=PACK))
        word_table = keep.tile([P, T], U32, align_bytes=64)
        nc.sync.dma_start(
            word_table[:].bitcast(I32), x_words[0].rearrange("p n t -> p (n t)").bitcast(I32)
        )
        load_list("n3", n3)
        load_list("n2", n2)

        half = keep.tile([P, 1], F32)
        nc.gpsimd.memset(half[:], 0.5)
        warm = keep.tile([P, 1], F32)
        nc.scalar.activation(warm[:], half[:], ACT.Abs_reciprocal_sqrt, bias=half[:])
        h_rows = []
        for m in range(TILES):
            h_row = keep.tile([P, S + SPARE], F32, name="h_row%d" % m)
            nc.gpsimd.memset(h_row[:, S:], 0.0)
            h_rows.append(h_row)

        picked_scales = keep.tile([P, S], U8, align_bytes=64, tag="picked_scales")
        nc.vector.tensor_copy(picked_scales[:], scale_table[:].indirect(lists["offs"][:]))
        x_plane = keep.tile([P, S], U8, align_bytes=64)
        nc.vector.memset(x_plane[:].bitcast(I32), 0)
        for q in range(4):
            rows = slice(32 * q, 32 * q + 1)
            nc.vector.tensor_copy(x_plane[rows, :].bitcast(I32), picked_scales[rows, :].bitcast(I32))
        for row in range(1, 4):
            nc.sync.dma_start(
                x_plane[row:P:32, :].bitcast(I32),
                picked_scales[8 * row : P : 32, :].bitcast(I32),
            )

        w2_rows = w2.rearrange("(p j) c -> p j c", j=PACK)
        w2_raw = keep.tile([P, 2, PACK, 2 * P], F32, align_bytes=64, tag="scale_table")
        for b in range(2):
            nc.sync.dma_start(w2_raw[:, b], w2_rows[:, :, b * 2 * P : (b + 1) * 2 * P])

        gain = keep.tile([P, PACK], F32, align_bytes=64, tag="picked_scales")
        nc.sync.dma_start(gain[:], gn.rearrange("(p t) o -> p (t o)", t=PACK))

        w1_bf = keep.tile([P, PACK * WIDTH], BF16, align_bytes=64)
        for copy, share in ((nc.scalar.copy, slice(0, 40)), (nc.vector.tensor_copy, slice(40, P))):
            copy(
                w1_bf[:].rearrange("p (t m j) -> p m j t", t=PACK, j=PACK)[:, share],
                w1_raw[:].rearrange("p j (m t) -> p m j t", t=PACK)[:, share],
            )
        w1_codes = keep.tile([P, WIDTH], U32, align_bytes=64)
        w1_plane = keep.tile([P, WIDTH], U8, align_bytes=64)
        nc.vector.quantize_mx(out=w1_codes[:].bitcast(FP8X4), scales=w1_plane[:], in_=w1_bf[:])

        x_codes = keep.tile([P, S], U32, align_bytes=64)
        nc.vector.tensor_copy(x_codes[:], word_table[:].indirect(lists["offs"][:]))

        size = keep.tile([P, PACK, S], F32)
        y_banks = []
        for a in range(2):
            cols = slice(a * HALF, (a + 1) * HALF)
            y_bank = psum.tile([P, PACK, HALF], F32, name="y_bank%d" % a)
            for t in range(PACK):
                rows = slice(t * P, (t + 1) * P)
                nc.tensor.matmul_mx(
                    out=y_bank[:, t, :],
                    lhsT=w1_codes[:, rows].bitcast(FP8X4),
                    lhsT_scale=w1_plane[:, rows],
                    rhs=x_codes[:, cols].bitcast(FP8X4),
                    rhs_scale=x_plane[:, cols],
                    start=True,
                    stop=True,
                )
            nc.scalar.activation(size[:, :, cols], y_bank[:], ACT.Abs)
            y_banks.append(y_bank)

        root = keep.tile([P, PACK, S], F32, tag="root")
        factors = [keep.tile([P, S], F32, name="factor%d" % t) for t in range(PACK)]
        for t in range(PACK):
            if t % 2 == 0:
                width = HALF if t == 0 else S
                for first in range(0, S, width):
                    part = slice(first, first + width)
                    nc.scalar.activation(
                        root[:, t : t + 2, part],
                        size[:, t : t + 2, part],
                        ACT.Abs_reciprocal_sqrt,
                        bias=half[:],
                    )
            nc.vector.scalar_tensor_tensor(
                factors[t][:], root[:, t, :], gain[:, t : t + 1], root[:, t, :], ALU.mult, ALU.mult
            )

        w2_codes = keep.tile([P, WIDTH], U32, align_bytes=64)
        w2_plane = keep.tile([P, WIDTH], U8, align_bytes=64)

        def interleave_w2(copy, staged, first):
            for m in range(2):
                rows = slice(m * P, (m + 1) * P)
                copy(
                    staged[:, m * P : (m + 1) * P, :].rearrange("p (c i) j -> p c j i", i=4),
                    w2_raw[:, first // 2, :, rows].rearrange("p j (c i) -> p c j i", i=4),
                )

        def quantize_w2(staged, first):
            rows = slice(first * P, (first + 2) * P)
            nc.vector.quantize_mx(
                out=w2_codes[:, rows].bitcast(FP8X4),
                scales=w2_plane[:, rows],
                in_=staged[:].rearrange("p c j -> p (c j)"),
            )

        def second_product(m, cols):
            rows = slice(m * P, (m + 1) * P)
            nc.tensor.matmul_mx(
                out=h_banks[m][:, cols],
                lhsT=w2_codes[:, rows].bitcast(FP8X4),
                lhsT_scale=w2_plane[:, rows],
                rhs=z_codes[:, cols].bitcast(FP8X4),
                rhs_scale=z_plane[:, cols],
                start=True,
                stop=True,
            )

        w2_low = keep.tile([P, 2 * P, PACK], BF16, align_bytes=64)
        interleave_w2(nc.vector.tensor_copy, w2_low, 0)
        quantize_w2(w2_low, 0)
        w2_high = keep.tile([P, 2 * P, PACK], BF16, align_bytes=64)
        interleave_w2(nc.vector.tensor_copy, w2_high, 2)
        quantize_w2(w2_high, 2)

        z_codes = keep.tile([P, S], U32, align_bytes=64)
        z_plane = keep.tile([P, S], U8, align_bytes=64)
        h_banks = [psum.tile([P, S], F32, name="h_bank%d" % m) for m in range(TILES)]
        for a in range(2):
            cols = slice(a * HALF, (a + 1) * HALF)
            picked = keep.tile([P, PACK, HALF], F32, name="picked%d" % a, tag=("picked", "root")[a])
            for t in range(PACK):
                nc.scalar.activation(
                    picked[:, t, :],
                    factors[t][:].indirect(lists["n1"][:, a * 8 : (a + 1) * 8]),
                    ACT.Copy,
                )
            z_bf = keep.tile([P, HALF, PACK], BF16, align_bytes=64, name="z_bf")
            nc.vector.tensor_tensor(
                z_bf[:].rearrange("p (c i) t -> p c t i", i=4),
                y_banks[a][:].rearrange("p t (c i) -> p c t i", i=4),
                picked[:].rearrange("p t (c i) -> p c t i", i=4),
                ALU.mult,
            )
            nc.vector.quantize_mx(
                out=z_codes[:, cols].bitcast(FP8X4),
                scales=z_plane[:, cols],
                in_=z_bf[:].rearrange("p c t -> p (c t)"),
            )
            for m in range(TILES):
                second_product(m, cols)

        for m in range(TILES):
            copy = nc.scalar.copy if m < 2 else nc.vector.tensor_copy
            copy(h_rows[m][:, :S], h_banks[m][:])

        for m in range(TILES):
            h_own = h_rows[m][:, :S]
            above = keep.tile([P, S], F32, name="above%d" % m)
            nc.scalar.activation(above[:], h_rows[m][:].indirect(lists["n3"][:]), ACT.Copy)
            rise = keep.tile([P, S], F32, name="rise%d" % m)
            nc.vector.tensor_tensor(rise[:], above[:], h_own, ALU.subtract)
            pull = keep.tile([P, S], F32, name="pull%d" % m)
            nc.vector.tensor_scalar(pull[:], rise[:], 0.0, 0.5, ALU.max, ALU.mult)
            below = keep.tile([P, S], F32, name="below%d" % m)
            drop = keep.tile([P, S], F32, name="drop%d" % m)
            result = keep.tile([P, S], F32, name="result%d" % m)
            window = h_rows[m][:]
            if m == 0:
                nc.scalar.activation(below[:, :HALF], window.indirect(lists["n2"][:, :8]), ACT.Copy)
                nc.vector.tensor_copy(below[:, HALF:], window.indirect(lists["n2"][:, 8:]))
            width = HALF if m == TILES - 1 else S
            for first in range(0, S, width):
                cols = slice(first, first + width)
                if m > 0:
                    entries = lists["n2"][:, first // 16 : (first + width) // 16]
                    nc.scalar.activation(below[:, cols], window.indirect(entries), ACT.Copy)
                nc.vector.tensor_tensor(drop[:, cols], h_own[:, cols], below[:, cols], ALU.subtract)
                nc.vector.scalar_tensor_tensor(
                    result[:, cols], drop[:, cols], 0.0, pull[:, cols], ALU.max, ALU.add
                )
                nc.sync.dma_start(out[m * P : (m + 1) * P, cols], result[:, cols])
